import numpy as np, ml_dtypes
CORES = [10,34,74,98]
N = 4
BF = ml_dtypes.bfloat16
def gentries(a):
    return np.ascontiguousarray(a.reshape(8, 16, -1).transpose(0, 2, 1)).reshape(8, -1)
def gtable(e):
    e = np.asarray(e); return np.ascontiguousarray(e.reshape(8, -1, 16).transpose(0, 2, 1)).reshape(128, -1).astype(np.int32)
V, D, T, RO, NEED = 2048, 2, 64, 2, 9
E = D * V
def graph(rng, sizes, kinds, stray):
    c = rng.choice(np.array(sizes), V); z = np.add.accumulate(c); i = np.arange(V)
    b = np.searchsorted(z, i, side="right"); a = (z - c)[b]; n = np.minimum(z[b], V) - a
    kind = rng.choice(np.array(kinds), V)[b]; back = a + np.where(kind == 2, rng.integers(0, n), 0)
    t = np.where(kind == 0, a + rng.integers(0, n, (D, V)), np.where(i + 1 < a + n, i + 1, back))
    t = np.where(rng.random((D, V)) < stray, rng.integers(0, V, (D, V)), t)
    line = rng.permutation(V); h = np.empty((D, V), np.int64); h[:, line] = line[t]
    q = np.empty((3, V), np.int64); q[:, line] = np.stack([b, i - a, n])
    return h, q
def spins(rng, lean):
    return np.minimum(np.maximum(rng.integers(-7, 8, (16, E)) + np.tile(lean, D), -7), 7)
def sevens(rng, *shape):
    return np.where(rng.random(shape) < 0.125, 6, 7)
def layers(rng, sizes, kinds, strays, step):
    x = np.empty((N, 8, 16, E), np.int64); h = np.empty((N, 8, D, V), np.int64)
    for r in range(N):
        for g in range(8):
            h[r, g], q = graph(rng, sizes, kinds, rng.choice(np.array(strays)))
            x[r, g] = spins(rng, rng.integers(-step, step + 1, V)[q[0]])
    return x, np.argsort(rng.random((N, 8, E)), axis=-1), h
def pack(x, o, h):
    s = np.empty((N, 8, 16, E), np.int64); np.put_along_axis(s, np.ascontiguousarray(np.broadcast_to(o[:, :, None, :], s.shape)), x, 3)
    e = np.empty((N, 8, E), np.int64); np.put_along_axis(e, o, h.reshape(N, 8, E), 2)
    return {"sp": s.reshape(N, 128, E).astype(np.float32).astype(BF), "lv": np.stack([gtable(a) for a in o]), "hd": e.astype(np.int32)}
SIZES = (1, 2, 3, 5, 8, 13, 21, 34, T, T + 9)
def setup_inputs(rng):
    return pack(*layers(rng, SIZES, (0, 0, 0, 1, 1, 2), (0.0, 0.01, 0.04), 2))
def setup_inputs_length(rng):
    x, o, h = layers(rng, (1, T // 2, T - 1, T, T, T + 1, T + 1, 2 * T, 3 * T), (1, 1, 2), (0.0,), 3)
    for r in (0, N - 1):
        for g, c in enumerate((T, T + 1, T - 1, 2 * T, T // 2 + 1, 2, 256 + T // 2)):
            h[r, g], q = graph(rng, (c,), (1,), 0.0); x[r, g] = spins(rng, np.full(V, 3))
        line = np.concatenate([np.zeros(1, np.int64), 1 + rng.permutation(V - 1)]); to = np.empty(V, np.int64)
        to[line[1:]] = line[:-1]; to[0] = line[rng.integers(0, T // 2)]
        h[r, 7] = to; x[r, 7] = rng.integers(1, 8, (16, E))
    return pack(x, o, h)
def setup_inputs_verdict(rng):
    x, o, h = layers(rng, (1,), (1,), (0.0,), 0)
    for r in range(N):
        for g in range(8):
            h[r, g], q = graph(rng, (1, 2, 3, 4, 5, 8, 16), (1,), 0.0); b, j, n = q
            amp = rng.integers(-6, 7, (16, V))[:, b]; y = np.where(j % 2 == 1, -amp, amp)
            y = np.where((n % 2 == 1) & (j == n - 1), 0, y)
            won = np.argsort(rng.random((16, V)), axis=0) < rng.choice(np.array([NEED - 1, NEED, NEED, 0, 16]), V)
            want = np.where(won, 1, -rng.integers(0, 2, (16, V)))[:, b]
            x[r, g] = np.tile(y + np.where(j == 0, want, 0), (1, D))
    return pack(x, o, h)
def setup_inputs_ties(rng):
    x, o, h = layers(rng, (1, 2, 3, 5, 8), (0, 0, 1), (0.0, 0.01), 0)
    x[:, :2] = rng.choice(np.array([-7, -1, 0, 1, 2]), (N, 2, 1, E)); x[:, 2:4] = rng.integers(-1, 2, (N, 2, 16, E))
    x[:, 4:] = rng.integers(5, 8, (N, 4, 16, E)); near = np.array([7] * 6 + [5] * 7 + [6] * 3)
    for g in range(4, 8):
        y = x[:, g]; v = rng.permutation(V)[:V // 16]
        y[:, :, v] = 6; y[:, :, V + v] = rng.permutation(near)[:, None]
        for k in range(2, D): y[:, :, k * V + v] = 5
    x[:, 5::2] = -x[:, 5::2]
    return pack(x, o, h)
def setup_inputs_alike(rng):
    x, o, h = layers(rng, SIZES, (0, 1, 2), (0.0, 0.02), 2); i = np.arange(V)
    h[:, 0] = i; h[:, 1] = i ^ 1; h[:, 2] = 0; h[:, 3] = V - 1; h[:, 4] = np.roll(i, -1); h[:, 5] = rng.choice(np.array([0, V - 1]), (N, D, V))
    o[:, 6] = np.arange(E); o[:, 7] = np.arange(E)[::-1]
    r = int(rng.integers(0, N)); h[r] = i
    x[r] = sevens(rng, 8, 16, E); x[(r + 1) % N] = -sevens(rng, 8, 16, E); x[(r - 1) % N, :2] = sevens(rng, 2, 16, E)
    return pack(x, o, h)
def setup_inputs_spread(rng):
    x, o, h = layers(rng, (1, 2, 3, 4, 6, 9, 30), (0, 0, 1, 2), (0.0, 0.02), 0)
    size = rng.choice(np.array([0, 1, 1, 3, 7, 7]), (N, 8, 1, E)); sign = rng.choice(np.array([-1, 0, 1]), (N, 8, 1, E))
    v = np.rint((2 * rng.random((N, 8, 16, E)) - 1) * size).astype(np.int64)
    return pack(np.where(sign == 0, v, sign * np.abs(v)), o, h)
def check_inputs(d):
    bad = []; s = np.asarray(d["sp"]).astype(np.float32)
    if not (np.all(np.abs(s) <= 7) and np.all(s == np.rint(s))): bad.append("whole numbers of sp")
    if any(np.any(np.sort(gentries(a), axis=1) != np.arange(E)) for a in d["lv"]): bad.append("each edge once in lv")
    if np.min(d["hd"]) < 0 or np.max(d["hd"]) > V - 1: bad.append("range of hd")
    return bad
def reference(sp, lv, hd):
    s = sp.astype(np.float32).astype(np.int64).reshape(N, 8, 16, E); h = hd.astype(np.int64)
    o = np.stack([gentries(a) for a in lv]).astype(np.int64); me = np.arange(V); w = np.zeros((N, 8, 16, V), np.int64)
    for rnd in range(RO):
        so = np.take_along_axis(s, o[:, :, None, :], 3)
        a = np.add.reduce(so * np.roll(so, -1, axis=0), axis=2).reshape(N, 8, D, V)
        slot = np.argmax(a, axis=2) * V + me
        c = np.take_along_axis(o, slot, 2); nx = np.take_along_axis(h, c, 2)
        m = np.take_along_axis(so, slot[:, :, None, :], 3); low = nx; p = nx; n = 1
        while n < T:
            m = m + np.take_along_axis(m, p[:, :, None, :], 3); low = np.minimum(low, np.take_along_axis(low, p, 2)); p = np.take_along_axis(p, p, 2); n = 2 * n
        w = w + m
        r, g, v = np.nonzero((low == me) & (np.add.reduce((m > 0).astype(np.int64), axis=2) >= NEED))
        turn = np.zeros((N, 8, V), bool)
        for j in range(T):
            turn[r, g, v] = True; v = nx[r, g, v]
        r, g, v = np.nonzero(turn); u = nx[r, g, v]; e = c[r, g, v]
        o[r, g, slot[r, g, u]] = e; h[r, g, e] = v; s[r, g, :, e] = -s[r, g, :, e]
    return {"ys": s.reshape(N, 128, E).astype(np.float32).astype(BF), "yl": o.astype(np.float32), "yh": h.astype(np.float32), "yw": w.reshape(N, 128, V).astype(np.float32)}

from concourse.bass import DstId, RemoteDMATransfer
from concourse.mybir import AluOpType as A, ActivationFunctionType as F

NSIM = 112
f32, bf, i32, u16, f16 = "float32", "bfloat16", "int32", "uint16", "float16"


def _sb(n, d):
    return ("sbuf", [128, n], d)


SCRATCH = {
    "SP": _sb(4096, bf), "SO2": _sb(8192, bf), "NB2": _sb(8192, bf), "EW": _sb(4096, f32), "T2": _sb(8192, f32),
    "PR": _sb(4096, bf), "S2B": _sb(4096, bf), "XA": _sb(2048, f32), "XB": _sb(2048, f32), "Y": _sb(2048, f32),
    "M64": _sb(2048, f32), "MA": _sb(2048, bf), "MB": _sb(2048, bf), "QA": _sb(2048, bf), "QB": _sb(2048, bf),
    "U16": _sb(2048, f16), "SCI": _sb(4096, f32), "PK": _sb(2048, bf), "MC": _sb(2048, bf), "IB": _sb(512, bf),
    "LVI": _sb(256, i32), "HC": _sb(256, i32), "EI": _sb(256, i32), "TI": _sb(256, i32), "TJ": _sb(256, i32),
    "CT": _sb(2048, f32), "XI": _sb(144, f32), "SW": _sb(256, f32), "SH": _sb(256, f32), "PC": _sb(8, i32),
    "COL": _sb(8, f32), "OH": _sb(16, f32), "BI": _sb(8, f32), "WB": _sb(144, f32),
    "Wp": _sb(144, f32), "Wl": _sb(144, f32), "Wk": _sb(144, f32), "Wone": _sb(144, bf), "Wneg": _sb(144, bf),
    "Wv": _sb(144, bf), "Wn": _sb(144, bf), "Wc": _sb(144, bf), "Ws": _sb(144, bf), "ID": _sb(128, f32),
    "LV16": _sb(256, u16), "LC16": _sb(128, u16), "LB16": _sb(128, u16), "P16": _sb(768, u16), "LO16": _sb(128, u16),
    "VL16": _sb(640, u16), "L216": _sb(256, u16), "NL16": _sb(256, u16), "SC16": _sb(256, u16), "IV16": _sb(256, u16),
    "L2": _sb(256, f32), "DL": _sb(128, f32), "KW": _sb(128, f32), "TK": _sb(128, f32), "LL": _sb(256, f32),
    "OW": _sb(256, f32), "V5": _sb(640, f32), "BT": _sb(640, i32), "VF": _sb(640, f32), "LW": _sb(128, f32),
    "TT": _sb(128, i32), "UC": _sb(128, f32), "W1": _sb(256, f32), "W2": _sb(256, f32), "W3": _sb(128, f32),
    "CI": _sb(256, i32), "SGW": _sb(256, f32), "G16": _sb(256, f16), "H16": _sb(128, f16), "D0": _sb(128, f32),
    "NX": _sb(128, f32), "IVC": _sb(256, f32), "EE": _sb(256, f32), "YL": ("sbuf", [128, 8, 4, 16], f32),
}
for _j in range(8):
    SCRATCH["P%d" % _j] = ("psum", [128, 512], f32)
SEMAPHORES = (["cv", "cs", "cp", "cg", "sent", "arrl0", "arrl1"] + ["arr%d" % _j for _j in range(4)]
              + ["d%d" % _j for _j in range(80)])

PIECES = [(1024, "die"), (1536, "far"), (0, "direct"), (512, "direct")]
ORDER = [2, 3, 0, 1]
MAGIC = 12582912.0


def _bits(es):
    m = 0
    for e in es:
        m |= 1 << e
    return m


def _relays(T, topo):
    out = []
    n = len(T.cores)
    for r in range(n):
        src, dst = T.cores[r], T.cores[(r - 1) % n]
        die = [c for c in topo.cores_of(src) if topo.die(c) != topo.die(src) and topo.may_write(c, dst)
               and c not in T.cores][0]
        far = [c for c in range(NSIM) if topo.mates(topo.chip(c), topo.chip(dst)) and topo.die(c) == topo.die(src)
               and topo.may_write(src, c) and topo.may_write(c, dst) and c not in T.cores][0]
        out.append({"src": src, "dst": dst, "die": die, "far": far})
    return out


def _piece_engines(topo, rl, n):
    off = topo.engines(rl["src"], rl["dst"])
    way = PIECES[n][1]
    if way == "die":
        return [e for e in topo.engines(rl["src"], rl["die"]) if e not in off]
    if way == "far" or n == 3:
        return off[len(off) // 2:]
    return off[:len(off) // 2]


def _relay_program(g, core, T, topo):
    for rl in _relays(T, topo):
        for n, (c, way) in enumerate(PIECES):
            if way != "direct" and rl[way] == core:
                rid, pid, _ = topo.addr(rl["dst"])
                g.wait_ge(T.sem["arr%d" % n], len(_piece_engines(topo, rl, n)))
                g.remote_dma(T.QA[:, c:c + 512], T.QA[:, c:c + 512], T.sem["arr%d" % n], T.sem["sent"], pid, rid,
                             topo.mask(core, rl["dst"]))
                g.wait_ge(T.sem["sent"], len(topo.engines(core, rl["dst"])))


def rank_program(g, core, T, topo):
    rank = T.rank_of(core)
    if rank is None:
        _relay_program(g, core, T, topo)
        return
    rls = _relays(T, topo)
    mine, nexts = rls[rank], rls[(rank + 1) % len(T.cores)]
    Q = {"v": g.vector, "s": g.scalar, "p": g.tensor, "g": g, "y": g.sync}
    count = {}
    known = {q: {} for q in Q}
    acc = {}
    nd = [0]

    def is_bank(name):
        return SCRATCH.get(name, ("",))[0] == "psum"

    def deps(q, reads, writes):
        need = {}
        for kind, rs in (("r", reads), ("w", writes)):
            for name, lo, hi in rs:
                bank = is_bank(name)
                for lo2, hi2, k2, tok, q2 in acc.get(name, []):
                    if (bank or (lo < hi2 and lo2 < hi)) and (kind == "w" or k2 == "w" or (bank and q2 != q)):
                        need[tok[0]] = max(need.get(tok[0], 0), tok[1])
        for s in sorted(need):
            if known[q].get(s, 0) < need[s]:
                Q[q].wait_ge(T.sem[s], need[s])
                known[q][s] = need[s]

    def note(q, reads, writes, tok):
        for name, lo, hi in writes:
            acc[name] = [e for e in acc.get(name, []) if not (is_bank(name) or (lo <= e[0] and e[1] <= hi))]
            acc[name].append((lo, hi, "w", tok, q))
        for name, lo, hi in reads:
            acc.setdefault(name, []).append((lo, hi, "r", tok, q))

    def op(q, fn, reads, writes):
        deps(q, reads, writes)
        s = "c" + q
        count[s] = count.get(s, 0) + 1
        fn().then_inc(T.sem[s], 1)
        note(q, reads, writes, (s, count[s]))

    def dmas(q, pairs, reads, writes, add=False):
        deps(q, reads, writes)
        s = "d%d" % nd[0]
        nd[0] += 1
        for o, i in pairs:
            (g.dma_start(o, i, accum_op=A.add) if add else Q[q].dma_start(o, i)).then_inc(T.sem[s], 16)
        count[s] = 16 * len(pairs)
        note(q, reads, writes, (s, count[s]))

    def arrives(region, s, n):
        count[s] = n
        note("g", [], [region], (s, n))

    def ap(r):
        return T[r[0]][:, r[1]:r[2]] if isinstance(r, tuple) else r

    def src(a, off):
        return ap(a).indirect(ap(off)) if off else ap(a)

    def regs(*xs):
        return [x for x in xs if isinstance(x, tuple)]

    def col(name, j):
        return (name, j, j + 1)

    def H(name, h, base=0, w=64):
        return (name, base + w * h, base + w * h + w)

    def tt(out, a, b, o, off=None):
        op("v", lambda: g.vector.tensor_tensor(ap(out), src(a, off), ap(b), o), regs(a, b, off), [out])

    def ts(out, a, s1, o1, s2=None, o2=None, off=None):
        ops = (o1,) if o2 is None else (o1, o2)
        op("v", lambda: g.vector.tensor_scalar(ap(out), src(a, off), ap(s1), ap(s2), *ops), regs(a, s1, s2, off), [out])

    def cp(out, a, off=None):
        op("v", lambda: g.vector.tensor_copy(ap(out), src(a, off)), regs(a, off), [out])

    def act(out, a, func=None, bias=None, scale=None, off=None):
        kw = {}
        if bias is not None:
            kw["bias"] = ap(bias)
        if scale is not None:
            kw["scale"] = ap(scale)
        fn = func if func is not None else (F.Identity if bias is not None or isinstance(scale, tuple) else F.Copy)
        op("s", lambda: g.scalar.activation(ap(out), src(a, off), fn, **kw), regs(a, bias, scale, off), [out])

    def gather(q, out, win, off, bias=None):
        if q == "s":
            act(out, win, bias=bias, off=off)
        else:
            cp(out, win, off)

    def iota(out, pattern, base, mult, integer=False):
        if integer:
            op("g", lambda: g.iota(ap(out), pattern, base, mult), [], [out])
        else:
            op("g", lambda: g.iota(ap(out), pattern, base, mult, allow_small_or_imprecise_dtypes=True), [], [out])

    def wrap(out, w, buf, c0, first=True, final=True):
        def fn():
            ins = None
            for i in range(16):
                ins = g.tensor.matmul(ap(out), T[w][:, 15 - i:143 - i], T[buf][:, c0 + i:c0 + 1024:16],
                                      first and i == 0, final and i == 15)
            return ins
        op("p", fn, [(w, 0, 144), (buf, c0, c0 + 1024)], [out])

    def unwrap_blocks(bank, a, j):
        def fn():
            ins = None
            for t in range(4):
                ins = g.tensor.matmul(ap(H(bank, t, 0, 128)), ap(H("U16", 4 * j + t, 0, 128)), ap(a), True, True)
            return ins
        op("p", fn, [("U16", 0, 2048), a], [(bank, 0, 512)])

    def unwrap_plain(bank, a):
        def fn():
            ins = None
            for i in range(16):
                ins = g.tensor.matmul(T[bank][:, i:512:16], ap(H("U16", i, 0, 128)), ap(a), True, True)
            return ins
        op("p", fn, [("U16", 0, 2048), a], [(bank, 0, 512)])

    def mix(bank, j0, a, j1, b):
        def fn():
            g.tensor.matmul(T[bank][:], ap(H("IB", j0, 0, 128)), ap(a), True, False)
            return g.tensor.matmul(T[bank][:], ap(H("IB", j1, 0, 128)), ap(b), False, True)
        op("p", fn, [("IB", 0, 512), a, b], [(bank, 0, 512)])

    VW = ("SW", 0, 128)

    dmas("y", [(T.LVI[:], T.lv[:])], [], [("LVI", 0, 256)])
    dmas("s", [(T.HC[:], T.hd[:])], [], [("HC", 0, 256)])
    dmas("y", [(T.SP[:, 0:2048], T.sp[:, 0:2048])], [], [("SP", 0, 2048)])
    dmas("s", [(T.SP[:, 2048:4096], T.sp[:, 2048:4096])], [], [("SP", 2048, 4096)])
    iota(("PC", 0, 1), [[0, 1]], 0, 1, True)
    iota(("XI", 0, 144), [[1, 144]], 0, 0)
    iota(("EI", 0, 256), [[1, 256]], 0, 256, True)
    iota(("CT", 1280, 1536), [[0, 4], [1, 64]], 0, 0)
    iota(("EW", 2560, 4096), [[0, 1536]], 0, 0)
    iota(("SW", 0, 256), [[16, 256]], 0, 0)
    op("v", lambda: g.vector.memset(T.EW[:, 0:1280], 0.0), [], [("EW", 0, 1280)])
    act(("EW", 1280, 2560), ("EW", 0, 1280))
    ts(col("PC", 1), col("PC", 0), 15, A.bitwise_and)
    cp(("COL", 0, 2), ("PC", 0, 2))
    ts(col("COL", 2), col("COL", 0), col("COL", 1), A.subtract, 15.0, A.add)
    ts(("OH", 0, 16), ("XI", 0, 16), col("COL", 1), A.is_equal)
    ts(("WB", 0, 144), ("XI", 0, 144), col("COL", 2), A.is_equal)
    ts(col("COL", 6), col("COL", 1), 3.0, A.is_ge, -128.0, A.mult)
    ts(("ID", 0, 128), ("XI", 0, 128), col("COL", 0), A.is_equal)
    for j, val in enumerate((1.0, 0.0625, 16.0, -16.0)):
        act(H("IB", j, 0, 128), ("ID", 0, 128), scale=val)
    for w, val in (("Wone", 1.0), ("Wneg", -1.0)):
        act((w, 0, 144), ("WB", 0, 144), scale=val)
    act(("Wp", 0, 144), ("WB", 0, 144), scale=col("OH", 2))
    ts(("TI", 0, 256), ("EI", 0, 256), 6, A.arith_shift_right, 63, A.bitwise_and)
    cp(("CT", 1024, 1280), ("TI", 0, 256))
    cp(("LV16", 0, 256), ("LVI", 0, 256))
    ts(("TI", 0, 256), ("HC", 0, 256), 6, A.arith_shift_right)
    ts(("TJ", 0, 256), ("HC", 0, 256), 63, A.bitwise_and)
    ts(("CT", 0, 256), ("HC", 0, 256), 64.0, A.mult)
    cp(("CT", 256, 512), ("HC", 0, 256))
    cp(("CT", 512, 768), ("TI", 0, 256))
    cp(("CT", 768, 1024), ("TJ", 0, 256))
    dmas("y", [(T.EW[r::16, :], T.CT[:, 256 * t:256 * t + 256]) for r, t in enumerate((0, 1, 1, 2, 3, 4, 5))],
         [("CT", 0, 1536)], [("EW", 0, 4096)])

    drid, dpid, _ = topo.addr(mine["dst"])
    sent = [0]

    def send(ns):
        deps("g", [("PK", PIECES[n][0], PIECES[n][0] + 512) for n in ns], [])
        tr = []
        for n in ns:
            c, way = PIECES[n]
            rid, pid, _ = topo.addr(mine["dst"] if way == "direct" else mine[way])
            es = _piece_engines(topo, mine, n)
            tr.append(RemoteDMATransfer(dst_ids=[DstId(rid=rid, pnc=pid)], dma_engine_mask=_bits(es),
                                        remote_sem=T.sem["arr%d" % n], src=T.PK[:, c:c + 512], dst=T.QA[:, c:c + 512]))
            sent[0] += len(es)
        g.remote_dma_fused(tr, local_sem=T.sem["sent"])

    def own(q, n, k):
        c = PIECES[n][0] + 2048 * k
        gather(q, ("SO2", c, c + 512), ("SP", 0, 4096), ("LV16", c // 16, c // 16 + 32))

    def pack(n):
        c = PIECES[n][0]
        mix("P%d" % (4 + n), 0, ("SO2", c, c + 512), 1, ("SO2", 2048 + c, 2560 + c))
        cp(("PK", c, c + 512), ("P%d" % (4 + n), 0, 512))

    own("v", 0, 0)
    own("s", 0, 1)
    own("v", 1, 0)
    own("s", 1, 1)
    pack(0)
    pack(1)
    send((0, 1))
    own("s", 2, 0)
    own("s", 2, 1)
    own("v", 3, 0)
    own("s", 3, 1)
    pack(2)
    pack(3)
    send((2, 3))
    for n, (c, way) in enumerate(PIECES):
        arrives(("QA", c, c + 512), "arr%d" % n,
                len(_piece_engines(topo, nexts, n)) if way == "direct" else len(topo.engines(nexts[way], core)))
    iota(("QB", 0, 2048), [[1, 16], [16, 8], [0, 16]], 0, 0)
    iota(("SH", 0, 256), [[1024, 2], [2048, 2], [16, 64]], 0, 0)
    iota(("V5", 0, 640), [[1024, 2], [0, 5], [16, 64]], 0, 0)
    iota(("T2", 4096, 8192), [[0, 2], [1, 2048]], 0, 0)
    iota(("SCI", 0, 2048), [[1, 128], [128, 16]], 64, 0)
    iota(("SCI", 2048, 4096), [[1, 2048]], 64 + 2048, 0)
    for j in range(4):
        gather("s", H("T2", j, 0, 1024), ("EW", 0, 4096), H("LV16", j))
    dmas("y", [(T.T2[7::16, 0:4096], T.CT[:, 1024:1280]), (T.T2[8::16, 0:4096], T.CT[:, 1280:1536])],
         [("CT", 1024, 1536)], [("T2", 0, 4096)])
    ts(col("COL", 7), col("OH", 2), 4096.0, A.mult, col("COL", 6), A.add)
    for b in range(5):
        ts(col("BI", b), col("OH", 0), float(2 ** b), A.mult, col("COL", 7), A.add)
    ts(col("BI", 5), col("OH", 0), 32.0, A.mult, col("COL", 6), A.subtract)
    ts(col("BI", 6), col("OH", 7), 64.0, A.mult, 640.0, A.add)
    ts(("SW", 0, 256), ("SW", 0, 256), col("COL", 1), A.add)
    op("v", lambda: g.vector.memset(T.DL[:], 2048.0), [], [("DL", 0, 128)])
    cp(("OW", 0, 256), ("LVI", 0, 256))
    ts(("TI", 0, 256), ("EI", 0, 256), 2047, A.bitwise_and)
    ts(("TJ", 0, 256), ("EI", 0, 256), 6, A.arith_shift_right, 31, A.bitwise_and)
    ts(("CT", 1536, 1792), ("TI", 0, 256), 64.0, A.mult)
    cp(("CT", 1792, 2048), ("TJ", 0, 256))
    dmas("y", [(T.T2[0::16, 4096:8192], T.CT[:, 1536:1792]), (T.T2[3::16, 4096:8192], T.CT[:, 1792:2048]),
               (T.T2[4::16, 4096:8192], T.CT[:, 1280:1536]), (T.T2[5::16, 4096:8192], T.T2[5::16, 0:4096]),
               (T.T2[6::16, 4096:8192], T.T2[6::16, 0:4096])],
         [("CT", 1280, 2048), ("T2", 0, 4096)], [("T2", 4096, 8192)])
    act(("Wv", 0, 144), ("WB", 0, 144), scale=16384.0)
    for w, r in (("Wk", 0), ("Wl", 1)):
        act((w, 0, 144), ("WB", 0, 144), scale=col("OH", r))
    for j, (w, r) in enumerate((("Wn", 3), ("Wc", 5), ("Ws", 7))):
        act(col("COL", 3 + j), col("OH", r), scale=64.0, bias=col("OH", r + 1))
        act((w, 0, 144), ("WB", 0, 144), scale=col("COL", 3 + j))
    X = ["XA", "XB"]
    QQ = ["QA", "QB"]

    for rnd in range(2):
        last = rnd == 1
        wn = 8192 if last else 4096

        def choice(h):
            ts(H("KW", h), ("P%d" % h, 0, 64), 0.0, A.is_gt)
            tt(H("TK", h), H("KW", h), H("DL", h), A.mult)
            tt(H("LL", h), H("TK", h), H("L2", 2 * h) if last else H("SW", h), A.add)
            cp(H("LC16", h), H("LL", h))

        def fix(b, h):
            act(H("Y", h, 0, 1024), H(X[b % 2], h, 0, 1024), bias=col("BI", b))

        def pbank(b, h):
            return H("P%d" % (6 + h), b) if b < 5 else ("P%d" % (2 + h), 0, 64)

        def pwrap(b, h):
            wrap(pbank(b, h), "Wl" if b == 6 else "Wp", X[b % 2], 1024 * h)

        def plist(b, h):
            cp(H("LO16", h) if b == 6 else H("P16", h, 128 * b), pbank(b, h))
            if b == 6:
                ts(H("LW", h), pbank(b, h), 64.0, A.mult, 31.0, A.add)

        def mstep(b, h):
            tt(H(X[(b + 1) % 2], h, 0, 1024), (X[b % 2], 0, 2048), H("Y", h, 0, 1024), A.min, off=H("P16", h, 128 * b))

        def shadow(r):
            dmas("y", [(ap(("MC", r[1], r[2])), ap(r))], [r], [("MC", r[1], r[2])])

        mdone = [0]

        def mq(n):
            for _ in range(n):
                b, qd = divmod(mdone[0], 4)
                new = H("M64" if b == 5 else ("MA" if b % 2 else "MB"), qd, 0, 512)
                tt(new, ("MB" if b % 2 else "MA", 0, 2048), H("MC", qd, 0, 512), A.add, off=H("P16", qd, 128 * b, 32))
                mdone[0] += 1
                if b < 5:
                    shadow(new)
                elif qd % 2:
                    c = 512 * (qd - 1)
                    dmas("g" if last else "y", [(T.yw[:, c:c + 1024], T.M64[:, c:c + 1024])], [("M64", c, c + 1024)],
                         [("yw", c, c + 1024)], add=last)

        sdone = [0]

        def bg(n):
            for _ in range(n):
                j = sdone[0]
                if last and j < 16:
                    op("s", lambda: g.scalar.activation(T.EW[:, 0:4096].indirect(T.SC16[:, 16 * j:16 * j + 16]),
                                                        T.SCI[:, 256 * j:256 * j + 256], F.Silu),
                       [("SC16", 0, 256), ("SCI", 0, 4096)], [("EW", 0, 4096)])
                    if j == 15:
                        dmas("s", [(T.IVC[:], T.EW[0::16, :])], [("EW", 0, 4096)], [("IVC", 0, 256)])
                elif not last and j < 8:
                    w, c = ("NB2", "SO2")[j // 4], 1024 * (j % 4)
                    act((w, 4096 + c, 5120 + c), (w, c, c + 1024), scale=-1.0)
                elif not last and j == 8:
                    act(("SH", 0, 256), ("SH", 0, 256), bias=col("COL", 1))
                    act(("V5", 0, 640), ("V5", 0, 640), bias=col("COL", 1))
                sdone[0] += 1

        def first_half():
            choice(0)
            gather("s", ("XA", 0, 1024), ("T2", 0, wn), H("LC16", 0))
            fix(0, 0)

        def dwrap(h, k):
            wrap(("P%d" % h, 0, 64), "Wone" if k else "Wneg", "PR", 2048 * k + 1024 * h, k == 0, k == 1)

        if last:
            for h in range(2):
                for k in range(2):
                    c = 2048 * k + 1024 * h
                    tt(("PR", c, c + 1024), ("NB2", 0, 8192), ("S2B", c, c + 1024), A.mult, off=H("NL16", 2 * h + k))
                    dwrap(h, k)
                    if h == 1 and k == 0:
                        first_half()
        else:
            def unpack(j):
                c = PIECES[ORDER[j]][0]
                ts(("NB2", c, c + 512), ("QA", c, c + 512), MAGIC, A.add, MAGIC, A.subtract)
                mix("P%d" % (4 + j), 2, ("QA", c, c + 512), 3, ("NB2", c, c + 512))
                act(("NB2", 2048 + c, 2560 + c), ("P%d" % (4 + j), 0, 512))

            def product(j, k):
                a = PIECES[ORDER[j]][0] + 2048 * k
                tt(("PR", a, a + 512), ("SP", 0, 4096), ("NB2", a, a + 512), A.mult, off=("LV16", a // 16, a // 16 + 32))
                if j % 2:
                    dwrap(j // 2, k)

            unpack(0)
            product(0, 0)
            ts(("U16", 0, 2048), ("QB", 0, 2048), col("COL", 0), A.is_equal)
            product(0, 1)
            unpack(1)
            product(1, 0)
            unpack(2)
            product(1, 1)
            product(2, 0)
            unpack(3)
            product(2, 1)
            first_half()
            product(3, 0)
            product(3, 1)
        pwrap(0, 0)
        choice(1)
        gather("s", ("XA", 1024, 2048), ("T2", 0, wn), H("LC16", 1))
        pwrap(0, 1)
        fix(0, 1)
        gather("v", ("MA", 0, 1024), ("SO2", 0, wn), H("LC16", 0))
        gather("s", ("MA", 1024, 2048), ("SO2", 0, wn), H("LC16", 1))
        shadow(("MA", 0, 1024))
        shadow(("MA", 1024, 2048))
        plist(0, 0)
        for b in range(6):
            mstep(b, 0)
            pwrap(b + 1, 0)
            if b < 5:
                fix(b + 1, 0)
            if b == 0 and last:
                tt(("W1", 0, 128), ("OW", 128, 256), ("OW", 0, 128), A.subtract)
                tt(("W1", 0, 128), ("W1", 0, 128), ("KW", 0, 128), A.mult)
                tt(("CI", 0, 128), ("OW", 0, 128), ("W1", 0, 128), A.add)
                tt(("CI", 128, 256), ("OW", 128, 256), ("W1", 0, 128), A.subtract)
            if b > 0:
                bg(2 if b == 5 else 1)
            plist(b, 1)
            mstep(b, 1)
            pwrap(b + 1, 1)
            if b < 5:
                fix(b + 1, 1)
            if b == 0 and last:
                ts(("TI", 0, 256), ("CI", 0, 256), 4, A.arith_shift_right)
                ts(("W1", 0, 256), ("TI", 0, 256), -4095.0 / 256.0, A.mult)
                tt(("W1", 0, 256), ("W1", 0, 256), ("CI", 0, 256), A.add)
                ts(("SC16", 0, 256), ("W1", 0, 256), 256.0, A.mult)
            elif b < 5:
                mq(1)
            bg(2 if b == 5 else 1)
            plist(b + 1, 0)
        gather("s", ("XB", 0, 1024), ("XA", 0, 2048), H("LO16", 0))
        if last:
            for h in range(2):
                tt(H("LL", h, 128), H("L2", 2 * h + 1), H("TK", h), A.subtract)
            cp(("LB16", 0, 128), ("LL", 128, 256))
            ts(("SGW", 0, 256), ("LL", 0, 256), 4096.0, A.is_lt, 0.5, A.subtract)
            cp(("G16", 128, 256), ("SGW", 128, 256))
            mq(1)
        else:
            mq(2)
        bg(1)
        plist(6, 1)
        gather("s", ("XB", 1024, 2048), ("XA", 0, 2048), H("LO16", 1))
        for h in range(2):
            wrap(("P%d" % h, 0, 64), "Wk", "XB", 1024 * h)
        bg(2)
        if last:
            gather("s", ("SCI", 2048, 3072), ("T2", 0, 8192), H("LB16", 0))
        for h in range(2):
            dd = ("P%d" % (6 + h), 0, 320)
            tt(dd, dd, H("V5", h, 0, 320), A.subtract)
        mq(2)
        for h in range(2):
            tt(H("TT", h), H("LW", h), ("P%d" % h, 0, 64), A.subtract)
            for b in range(5):
                ts(H("BT", 5 * h + b), H("TT", h), b, A.arith_shift_right, 1, A.bitwise_and)
            dd = ("P%d" % (6 + h), 0, 320)
            tt(dd, H("BT", h, 0, 320), dd, A.mult)
            tt(H("VF", h, 0, 320), dd, H("V5", h, 0, 320), A.add)
            cp(H("VL16", h, 0, 320), H("VF", h, 0, 320))

        def level(b, h, q):
            gather(q, H(QQ[b % 2], h, 0, 1024), ("XA" if b == 0 else QQ[(b + 1) % 2], 0, 2048), H("VL16", 5 * h + b),
                   bias=col("BI", 6) if b == 0 else None)

        def vote(h, q, out):
            if q == "v":
                ts(H("MA", h, 0, 1024), ("M64", 0, 2048), 0.0, A.is_gt, 0.5, A.subtract, off=H("LO16", h))
            else:
                act(H("MA", h, 0, 1024), ("M64", 0, 2048), func=F.Sign, bias=-0.5, off=H("LO16", h))
            wrap(out, "Wv", "MA", 1024 * h)

        level(0, 0, "s")
        if last:
            gather("s", ("SCI", 3072, 4096), ("T2", 0, 8192), H("LB16", 1))
        level(0, 1, "s")
        for b in range(1, 4):
            level(b, 0, "s")
            level(b, 1, "s")
        level(4, 0, "s")

        def check_value():
            ts(("TI", 0, 128), ("TT", 0, 128), 5, A.arith_shift_right)
            ts(("W1", 0, 128), ("TI", 0, 128), 4096.0, A.mult)
            tt(("UC", 0, 128), ("W1", 0, 128), VW, A.add)

        def turned_values():
            ts(("W3", 0, 128), ("SGW", 0, 128), -2.0, A.mult)
            cp(("NX", 0, 128), ("P16", 0, 128))
            tt(("D0", 0, 128), ("NX", 0, 128), VW, A.subtract)

        def positions():
            cp(("TJ", 0, 256), ("IVC", 0, 256))
            ts(("IV16", 0, 256), ("TJ", 0, 256), -64.0, A.add)

        between = [check_value] + ([turned_values, positions] if last else [])
        if last:
            for j in range(4):
                unwrap_plain("P%d" % (4 + j), H("G16", j, 128, 32))
        while mdone[0] < 24:
            mq(1)
            if mdone[0] % 4 == 1 and between:
                between.pop(0)()
        if not last:
            level(4, 1, "s")
            for h in range(2):
                wrap(H("P%d" % (2 + h), 0), "Wn", "QA", 1024 * h)
                wrap(H("P%d" % (2 + h), 1), "Ws", "QA", 1024 * h)
                vote(h, "vs"[h], H("P%d" % h, 0))
            for h in range(2):
                z, a0, a1 = H("P%d" % h, 0), H("W1", 2 * h), H("W1", 2 * h + 1)
                tt(a0, H("P%d" % (2 + h), 0), H("UC", h), A.is_equal)
                tt(a0, H("P%d" % (2 + h), 1), a0, A.mult)
                tt(a1, a0, H("KW", h), A.mult)
                tt(a0, a0, a1, A.subtract)
                tt(H("P5", 0), z, a0, A.min)
                tt(H("P5", 1), z, a1, A.min)
                tt(H("L2", h, 0, 128), ("P5", 0, 128), H("SH", h, 0, 128), A.max)
                cp(H("L216", h, 0, 128), H("L2", h, 0, 128))
                deps("g", [H("L216", h, 0, 128)], [])
                g.remote_dma(ap(H("NL16", h, 0, 128)), ap(H("L216", h, 0, 128)), T.sem["arrl%d" % h], T.sem["sent"],
                             dpid, drid, topo.mask(core, mine["dst"]))
                sent[0] += len(topo.engines(core, mine["dst"]))
                arrives(H("NL16", h, 0, 128), "arrl%d" % h, len(topo.engines(nexts["src"], core)))
                for k in range(2):
                    c = 2048 * k + 1024 * h
                    gather("s", ("S2B", c, c + 1024), ("SO2", 0, 8192), H("L216", 2 * h + k))
            for h in range(2):
                wrap(H("P4", h), "Wc", "QA", 1024 * h)
            for h in range(2):
                tt(H("DL", h), H("L2", 2 * h + 1), H("L2", 2 * h), A.subtract)
                for k in range(2):
                    ts(H("W1", 2 * k + h), H("L2", 2 * h + k), 4096.0, A.is_ge)
            for k in range(2):
                tt(H("W2", k, 0, 128), ("P4", 0, 128), H("OW", k, 0, 128), A.subtract)
            tt(("W1", 0, 256), ("W1", 0, 256), ("W2", 0, 256), A.mult)
            tt(("OW", 0, 256), ("OW", 0, 256), ("W1", 0, 256), A.add)
            continue
        level(4, 1, "v")
        wrap(H("P2", 0), "Wn", "QA", 0)
        wrap(H("P1", 0), "Wc", "QA", 0)
        vote(1, "s", H("P0", 1))
        wrap(H("P2", 1), "Wn", "QA", 1024)
        wrap(H("P1", 1), "Wc", "QA", 1024)
        vote(0, "v", H("P0", 0))
        for j in range(4):
            act(H("S2B", j, 2048, 512), ("P%d" % (4 + j), 0, 512), scale=2.0)
        tt(("W1", 0, 128), ("P2", 0, 128), ("UC", 0, 128), A.is_equal)
        ts(("W1", 0, 128), ("W1", 0, 128), -1.0e6, A.mult, 1000000.5, A.add)
        tt(("W2", 0, 128), ("P0", 0, 128), ("W1", 0, 128), A.is_gt)
        tt(("W1", 0, 128), ("W2", 0, 128), ("W3", 0, 128), A.mult)
        tt(("G16", 0, 128), ("W1", 0, 128), ("SGW", 0, 128), A.add)
        tt(("W1", 128, 256), ("W2", 0, 128), ("D0", 0, 128), A.mult)
        tt(("H16", 0, 128), ("NX", 0, 128), ("W1", 128, 256), A.subtract)
        tt(("EE", 0, 128), ("P1", 0, 128), ("CI", 0, 128), A.subtract)
        for j in range(4):
            unwrap_blocks("P%d" % (4 + j), ("G16", 0, 128), j)
            unwrap_blocks("P%d" % j, ("H16", 0, 128), j)
            ts(H("S2B", j, 0, 512), ("P%d" % (4 + j), 0, 512), 2.0, A.mult)
            act(H("SCI", j, 0, 512), ("P%d" % j, 0, 512))
        cuts = [0, 1280, 2560, 3584, 4096]
        for n in range(4):
            a, b = cuts[n], cuts[n + 1]
            tt(("PR", a, b), ("S2B", 0, 4096), ("SP", a, b), A.mult, off=("IV16", a // 16, b // 16))
            dmas("y", [(T.ys[:, a:b], T.PR[:, a:b])], [("PR", a, b)], [])
            if n == 0:
                tt(("EE", 0, 128), ("EE", 0, 128), ("W2", 0, 128), A.mult)
                tt(("EE", 128, 256), ("EE", 0, 128), ("KW", 0, 128), A.mult)
                tt(("EE", 0, 128), ("EE", 0, 128), ("EE", 128, 256), A.subtract)
                tt(("OW", 0, 256), ("OW", 0, 256), ("EE", 0, 256), A.add)

                def turn_over():
                    ins = None
                    for t in range(4):
                        ins = g.tensor.matmul(T.P4[0:64, 128 * t:128 * t + 128], T.OW[:, t:256:4], T.ID[:], True, True)
                    return ins
                op("p", turn_over, [("OW", 0, 256), ("ID", 0, 128)], [("P4", 0, 512)])
            gather("s", ("T2", a, b), ("SCI", 0, 4096), ("IV16", a // 16, b // 16))
            if n % 2:
                dmas("y", [(T.yh[:, cuts[n - 1]:b], T.T2[2::16, cuts[n - 1]:b])], [("T2", cuts[n - 1], b)], [])
            if n == 1:
                for t in range(4):
                    op("s", lambda: g.scalar.activation(T.YL[0:64, :, t, :], T.P4[0:64, 128 * t:128 * t + 128], F.Copy),
                       [("P4", 0, 512)], [("YL", t, t + 1)])
                dmas("y", [(T.yl[gg, :], T.YL[0:64, gg, :, :]) for gg in range(8)], [("YL", 0, 4)], [])
    count["sent"] = sent[0]
    for s in sorted(count):
        if known["g"].get(s, 0) < count[s]:
            g.wait_ge(T.sem[s], count[s])
